import numpy as np, ml_dtypes
CORES = [56,61,80,85]
N = 4
S, B = 3, 128
def setup_inputs(rng):
    a = (rng.standard_normal((128, 128), dtype=np.float32) / 12).astype(ml_dtypes.bfloat16)
    return {"x": rng.standard_normal((N, 128, S * B), dtype=np.float32).astype(ml_dtypes.bfloat16), "a": np.broadcast_to(a, (N, 128, 128)).copy(), "at": np.broadcast_to(a.T, (N, 128, 128)).copy()}
def setup_inputs_big(rng):
    d = setup_inputs(rng)
    for k in ("x",): d[k] = (d[k].astype(np.float32) * 1048576.0).astype(d[k].dtype)
    return d
def setup_inputs_small(rng):
    d = setup_inputs(rng)
    for k in ("x",): d[k] = (d[k].astype(np.float32) * (1 / 1048576.0)).astype(d[k].dtype)
    return d
def setup_inputs_apart(rng):
    d = setup_inputs(rng)
    f = (10.0 ** rng.permutation(np.linspace(-1.5, 1.5, N))).astype(np.float32).reshape(N, 1, 1)
    for k in ("x",): d[k] = (d[k].astype(np.float32) * f).astype(d[k].dtype)
    return d
def reference(x, a, at):
    X, A = x.astype(np.float64), a.astype(np.float64)
    y = np.zeros((N, 128, S * B)); h = np.zeros((128, B))
    for r in range(N):
        for s in range(S):
            h = A[r].T @ h + X[r][:, B * s:B * s + B]
            y[r][:, B * s:B * s + B] = h
    return {"y": y.astype(ml_dtypes.bfloat16)}

@@ -1,0 +1,180 @@
+from concourse.bass import DstId, RemoteDMATransfer
+from concourse.mybir import AluOpType
+
+B = 128
+ENG_CHIP = 8
+ENG_LINK = 4
+
+_BF = "bfloat16"
+SCRATCH = {
+    "xs": ("sbuf", [128, 3 * B], _BF),
+    "ats": ("sbuf", [128, B], _BF),
+    "pw": ("sbuf", [128, 7 * B], _BF),
+    "lb": ("sbuf", [128, 2 * B], _BF),
+    "d0": ("sbuf", [128, B], _BF),
+    "cin": ("sbuf", [128, B], _BF),
+    "hin": ("sbuf", [128, B], _BF),
+    "rl0": ("sbuf", [128, B], _BF),
+    "rl1": ("sbuf", [128, B], _BF),
+    "yb": ("sbuf", [128, 3 * B], _BF),
+    "pa": ("psum", [128, 512], "float32"),
+    "pb": ("psum", [128, 512], "float32"),
+    "pc": ("psum", [128, 512], "float32"),
+    "pd": ("psum", [128, 512], "float32"),
+    "py0": ("psum", [128, 512], "float32"),
+    "py1": ("psum", [128, 512], "float32"),
+    "py2": ("psum", [128, 512], "float32"),
+}
+SEMAPHORES = ["ld_x", "ld_a", "ld_at", "t_l1", "t_l2", "v_l1", "v_l2", "t_p1", "t_p2", "t_p3", "v_p1", "v_p2", "v_p3",
+              "t_d", "v_d", "t_y0", "t_y1", "t_y2", "v_y", "arr_c", "arr_h", "arr_r", "sent", "st"]
+
+_SLOT = {1: 0, 2: 1, 3: 3, 4: 4, 5: 5, 6: 6}
+
+
+def _engines(mask, n):
+    bits = [b for b in range(mask.bit_length()) if (mask >> b) & 1]
+    m = 0
+    for b in bits[::len(bits) // n][:n]:
+        m |= 1 << b
+    return m
+
+
+def _relays(cores, topo):
+    near = topo.chip(cores[1])
+    idle = [c for c in range(topo.CHIPS * topo.CORES_PER_CHIP) if topo.chip(c) == near and c not in cores]
+    out = []
+    for dst in cores[2:]:
+        ok = [c for c in idle if topo.may_write(c, dst) and c not in out]
+        same = [c for c in ok if topo.die(c) == topo.die(dst)]
+        out.append((same or ok)[0])
+    return out
+
+
+def _dst(topo, c):
+    rid, pid, _ = topo.addr(c)
+    return DstId(rid=rid, pnc=pid)
+
+
+def rank_program(g, core, T, topo):
+    cores = list(T.cores)
+    S = T.sem
+    relays = _relays(cores, topo)
+
+    if core in relays:
+        dst = cores[2 + relays.index(core)]
+        g.wait_ge(S.arr_r, 2 * ENG_CHIP)
+        g.remote_dma_fused([RemoteDMATransfer(
+            dst_ids=[_dst(topo, dst)], dma_engine_mask=_engines(topo.mask(core, dst), ENG_LINK), remote_sem=S.arr_h,
+            srcs=[T.rl0[:], T.rl1[:]], dsts=[T.hin[:]], alu_op=1)], local_sem=S.sent)
+        g.wait_ge(S.sent, ENG_LINK)
+        return
+
+    rank = T.rank_of(core)
+    if rank is None:
+        return
+    te, ve, sy, sc = g.tensor, g.vector, g.sync, g.scalar
+
+    def P(k, n=1):
+        return T.pw[:, _SLOT[k] * B:(_SLOT[k] + n) * B]
+
+    A = P(1)
+    AT2 = T.pw[:, 2 * B:3 * B]
+    l = [T.xs[:, 0:B], T.lb[:, 0:B], T.lb[:, B:2 * B]]
+    wide = rank == 3
+
+    sc.dma_start(T.xs[:], T.x[:]).then_inc(S.ld_x, 16)
+    sy.dma_start(A, T.a[:]).then_inc(S.ld_a, 16)
+    sy.dma_start(T.ats[:], T.at[:]).then_inc(S.ld_at, 16)
+
+    te.wait_ge(S.ld_a, 16)
+    te.wait_ge(S.ld_x, 16)
+    te.matmul(T.pa[:, 0:B], A, l[0], True, True).then_inc(S.t_l1, 1)
+    te.wait_ge(S.ld_at, 16)
+    te.matmul(T.pc[:, 0:B], T.ats[:], A, True, True).then_inc(S.t_p1, 1)
+    if wide:
+        te.matmul(T.pc[:, B:2 * B], A, T.ats[:], True, True).then_inc(S.t_p1, 1)
+    te.wait_ge(S.v_l1, 1)
+    te.matmul(T.pb[:, 0:B], A, l[1], True, True).then_inc(S.t_l2, 1)
+    te.wait_ge(S.v_p1, 1)
+    if wide:
+        te.matmul(T.pd[:, 0:2 * B], AT2, P(1, 2), True, True).then_inc(S.t_p2, 1)
+        te.wait_ge(S.v_p2, 1)
+        te.matmul(T.pa[:, 0:2 * B], AT2, P(3, 2), True, True).then_inc(S.t_p3, 1)
+        te.wait_ge(S.v_p3, 1)
+    else:
+        te.matmul(T.pd[:, 0:B], T.ats[:], P(2), True, True).then_inc(S.t_p2, 1)
+        te.wait_ge(S.v_p2, 1)
+
+    ve.wait_ge(S.ld_x, 16)
+    ve.wait_ge(S.t_l1, 1)
+    ve.tensor_tensor(l[1], T.pa[:, 0:B], T.xs[:, B:2 * B], AluOpType.add).then_inc(S.v_l1, 1)
+    w = 2 if wide else 1
+    ve.wait_ge(S.t_p1, w)
+    ve.tensor_copy(T.pw[:, B:(1 + w) * B], T.pc[:, 0:w * B]).then_inc(S.v_p1, 1)
+    ve.wait_ge(S.t_l2, 1)
+    ve.tensor_tensor(l[2], T.pb[:, 0:B], T.xs[:, 2 * B:3 * B], AluOpType.add).then_inc(S.v_l2, 1)
+    ve.wait_ge(S.t_p2, 1)
+    ve.tensor_copy(P(3, w), T.pd[:, 0:w * B]).then_inc(S.v_p2, 1)
+    if wide:
+        ve.wait_ge(S.t_p3, 1)
+        ve.tensor_copy(P(5, 2), T.pa[:, 0:2 * B]).then_inc(S.v_p3, 1)
+
+    def to_relays(src, land):
+        m = topo.mask(core, relays[0]) & topo.mask(core, relays[1])
+        g.remote_dma_fused([RemoteDMATransfer(
+            dst_ids=[_dst(topo, c) for c in relays], dma_engine_mask=_engines(m, ENG_CHIP), remote_sem=S.arr_r,
+            srcs=[src], dsts=[land, land], alu_op=0)], local_sem=S.sent)
+
+    def carry_to(dst):
+        rid, pid, _ = topo.addr(dst)
+        g.remote_dma(out_ap=T.cin[:], in_ap=l[2], remote_sem=S.arr_c, local_sem=S.sent, pid=pid, routing_id=rid,
+                     dma_engine_mask=_engines(topo.mask(core, dst), ENG_CHIP))
+
+    if rank == 0:
+        te.wait_ge(S.v_l2, 1)
+        te.matmul(T.py0[:, 0:B], P(3), l[2], True, True).then_inc(S.t_d, 1)
+        ve.wait_ge(S.t_d, 1)
+        ve.tensor_copy(T.d0[:], T.py0[:, 0:B]).then_inc(S.v_d, 1)
+        g.wait_ge(S.v_d, 1)
+        to_relays(T.d0[:], T.rl0[:])
+        g.wait_ge(S.v_l2, 1)
+        carry_to(cores[1])
+        g.wait_ge(S.sent, 2 * ENG_CHIP)
+        sy.wait_ge(S.sent, 2 * ENG_CHIP)
+        sy.wait_ge(S.ld_x, 16)
+        sy.wait_ge(S.v_l1, 1)
+        sy.wait_ge(S.v_l2, 1)
+        sy.dma_start(T.y[:, 0:B], l[0]).then_inc(S.st, 16)
+        sy.dma_start(T.y[:, B:3 * B], T.lb[:]).then_inc(S.st, 16)
+        sy.wait_ge(S.st, 32)
+        return
+
+    if rank == 1:
+        g.wait_ge(S.v_l2, 1)
+        to_relays(l[2], T.rl1[:])
+        g.wait_ge(S.sent, ENG_CHIP)
+    elif rank == 2:
+        g.wait_ge(S.v_l2, 1)
+        carry_to(cores[3])
+        g.wait_ge(S.sent, ENG_CHIP)
+
+    terms = {1: [(S.arr_c, ENG_CHIP, T.cin, 1)],
+             2: [(S.arr_h, ENG_LINK, T.hin, 1)],
+             3: [(S.arr_c, ENG_CHIP, T.cin, 1), (S.arr_h, ENG_LINK, T.hin, 4)]}[rank]
+    py = [T.py0, T.py1, T.py2]
+    ty = [S.t_y0, S.t_y1, S.t_y2]
+    for i, (sem, cnt, buf, p0) in enumerate(terms):
+        te.wait_ge(sem, cnt)
+        last = i == len(terms) - 1
+        for s in range(3):
+            mm = te.matmul(py[s][:, 0:B], P(p0 + s), buf[:], i == 0, last)
+            if last:
+                mm.then_inc(ty[s], 1)
+    ve.wait_ge(S.v_l1, 1)
+    ve.wait_ge(S.v_l2, 1)
+    for s in range(3):
+        ve.wait_ge(ty[s], 1)
+        ve.tensor_tensor(T.yb[:, s * B:(s + 1) * B], py[s][:, 0:B], l[s], AluOpType.add).then_inc(S.v_y, 1)
+    sy.wait_ge(S.v_y, 3)
+    sy.dma_start(T.y[:], T.yb[:]).then_inc(S.st, 16)
+    sy.wait_ge(S.st, 16)

@@ -3,7 +3,7 @@ from concourse.mybir import AluOpType
 
 B = 128
 ENG_CHIP = 8
-ENG_LINK = 4
+ENG_LINK = 8
 
 _BF = "bfloat16"
 SCRATCH = {
@@ -11,11 +11,14 @@ SCRATCH = {
     "ats": ("sbuf", [128, B], _BF),
     "pw": ("sbuf", [128, 7 * B], _BF),
     "lb": ("sbuf", [128, 2 * B], _BF),
+    "mb": ("sbuf", [128, B], _BF),
     "d0": ("sbuf", [128, B], _BF),
     "cin": ("sbuf", [128, B], _BF),
+    "cx": ("sbuf", [128, B], _BF),
     "hin": ("sbuf", [128, B], _BF),
     "rl0": ("sbuf", [128, B], _BF),
     "rl1": ("sbuf", [128, B], _BF),
+    "rlx": ("sbuf", [128, B], _BF),
     "yb": ("sbuf", [128, 3 * B], _BF),
     "pa": ("psum", [128, 512], "float32"),
     "pb": ("psum", [128, 512], "float32"),
@@ -25,8 +28,8 @@ SCRATCH = {
     "py1": ("psum", [128, 512], "float32"),
     "py2": ("psum", [128, 512], "float32"),
 }
-SEMAPHORES = ["ld_x", "ld_a", "ld_at", "t_l1", "t_l2", "v_l1", "v_l2", "t_p1", "t_p2", "t_p3", "v_p1", "v_p2", "v_p3",
-              "t_d", "v_d", "t_y0", "t_y1", "t_y2", "v_y", "arr_c", "arr_h", "arr_r", "sent", "st"]
+SEMAPHORES = ["ld_x", "ld_a", "ld_at", "t_l1", "t_l2", "v_l1", "v_l2", "v_m", "t_p1", "t_p2", "t_p3", "v_p1", "v_p2",
+              "v_p3", "t_d", "v_d", "t_y0", "t_y1", "t_y2", "v_y", "arr_c", "arr_h", "arr_r", "sent", "st"]
 
 _SLOT = {1: 0, 2: 1, 3: 3, 4: 4, 5: 5, 6: 6}
 
@@ -62,10 +65,10 @@ def rank_program(g, core, T, topo):
 
     if core in relays:
         dst = cores[2 + relays.index(core)]
-        g.wait_ge(S.arr_r, 2 * ENG_CHIP)
+        g.wait_ge(S.arr_r, 3 * ENG_CHIP)
         g.remote_dma_fused([RemoteDMATransfer(
             dst_ids=[_dst(topo, dst)], dma_engine_mask=_engines(topo.mask(core, dst), ENG_LINK), remote_sem=S.arr_h,
-            srcs=[T.rl0[:], T.rl1[:]], dsts=[T.hin[:]], alu_op=1)], local_sem=S.sent)
+            srcs=[T.rl0[:], T.rl1[:], T.rlx[:]], dsts=[T.hin[:]], alu_op=1)], local_sem=S.sent)
         g.wait_ge(S.sent, ENG_LINK)
         return
 
@@ -80,7 +83,9 @@ def rank_program(g, core, T, topo):
     A = P(1)
     AT2 = T.pw[:, 2 * B:3 * B]
     l = [T.xs[:, 0:B], T.lb[:, 0:B], T.lb[:, B:2 * B]]
+    xlast = T.xs[:, 2 * B:3 * B]
     wide = rank == 3
+    w = 2 if wide else 1
 
     sc.dma_start(T.xs[:], T.x[:]).then_inc(S.ld_x, 16)
     sy.dma_start(A, T.a[:]).then_inc(S.ld_a, 16)
@@ -105,14 +110,28 @@ def rank_program(g, core, T, topo):
         te.matmul(T.pd[:, 0:B], T.ats[:], P(2), True, True).then_inc(S.t_p2, 1)
         te.wait_ge(S.v_p2, 1)
 
+    def v_square():
+        ve.wait_ge(S.t_p1, w)
+        ve.tensor_copy(T.pw[:, B:(1 + w) * B], T.pc[:, 0:w * B]).then_inc(S.v_p1, 1)
+
+    def v_carry():
+        ve.wait_ge(S.t_l2, 1)
+        ve.tensor_tensor(l[2], T.pb[:, 0:B], xlast, AluOpType.add).then_inc(S.v_l2, 1)
+
+    def v_m():
+        ve.wait_ge(S.t_l2, 1)
+        ve.tensor_copy(T.mb[:], T.pb[:, 0:B]).then_inc(S.v_m, 1)
+
     ve.wait_ge(S.ld_x, 16)
     ve.wait_ge(S.t_l1, 1)
     ve.tensor_tensor(l[1], T.pa[:, 0:B], T.xs[:, B:2 * B], AluOpType.add).then_inc(S.v_l1, 1)
-    w = 2 if wide else 1
-    ve.wait_ge(S.t_p1, w)
-    ve.tensor_copy(T.pw[:, B:(1 + w) * B], T.pc[:, 0:w * B]).then_inc(S.v_p1, 1)
-    ve.wait_ge(S.t_l2, 1)
-    ve.tensor_tensor(l[2], T.pb[:, 0:B], T.xs[:, 2 * B:3 * B], AluOpType.add).then_inc(S.v_l2, 1)
+    if rank == 1:
+        v_m()
+        v_carry()
+        v_square()
+    else:
+        v_square()
+        v_carry()
     ve.wait_ge(S.t_p2, 1)
     ve.tensor_copy(P(3, w), T.pd[:, 0:w * B]).then_inc(S.v_p2, 1)
     if wide:
@@ -125,9 +144,10 @@ def rank_program(g, core, T, topo):
             dst_ids=[_dst(topo, c) for c in relays], dma_engine_mask=_engines(m, ENG_CHIP), remote_sem=S.arr_r,
             srcs=[src], dsts=[land, land], alu_op=0)], local_sem=S.sent)
 
-    def carry_to(dst):
+    def to_next(src, land):
+        dst = cores[rank + 1]
         rid, pid, _ = topo.addr(dst)
-        g.remote_dma(out_ap=T.cin[:], in_ap=l[2], remote_sem=S.arr_c, local_sem=S.sent, pid=pid, routing_id=rid,
+        g.remote_dma(out_ap=land, in_ap=src, remote_sem=S.arr_c, local_sem=S.sent, pid=pid, routing_id=rid,
                      dma_engine_mask=_engines(topo.mask(core, dst), ENG_CHIP))
 
     if rank == 0:
@@ -135,12 +155,15 @@ def rank_program(g, core, T, topo):
         te.matmul(T.py0[:, 0:B], P(3), l[2], True, True).then_inc(S.t_d, 1)
         ve.wait_ge(S.t_d, 1)
         ve.tensor_copy(T.d0[:], T.py0[:, 0:B]).then_inc(S.v_d, 1)
+        v_m()
+        g.wait_ge(S.ld_x, 16)
+        to_next(xlast, T.cx[:])
         g.wait_ge(S.v_d, 1)
         to_relays(T.d0[:], T.rl0[:])
-        g.wait_ge(S.v_l2, 1)
-        carry_to(cores[1])
-        g.wait_ge(S.sent, 2 * ENG_CHIP)
-        sy.wait_ge(S.sent, 2 * ENG_CHIP)
+        g.wait_ge(S.v_m, 1)
+        to_next(T.mb[:], T.cin[:])
+        g.wait_ge(S.sent, 3 * ENG_CHIP)
+        sy.wait_ge(S.sent, 3 * ENG_CHIP)
         sy.wait_ge(S.ld_x, 16)
         sy.wait_ge(S.v_l1, 1)
         sy.wait_ge(S.v_l2, 1)
@@ -150,26 +173,30 @@ def rank_program(g, core, T, topo):
         return
 
     if rank == 1:
-        g.wait_ge(S.v_l2, 1)
-        to_relays(l[2], T.rl1[:])
-        g.wait_ge(S.sent, ENG_CHIP)
+        g.wait_ge(S.ld_x, 16)
+        to_relays(xlast, T.rlx[:])
+        g.wait_ge(S.v_m, 1)
+        to_relays(T.mb[:], T.rl1[:])
+        g.wait_ge(S.sent, 2 * ENG_CHIP)
     elif rank == 2:
         g.wait_ge(S.v_l2, 1)
-        carry_to(cores[3])
+        to_next(l[2], T.cin[:])
         g.wait_ge(S.sent, ENG_CHIP)
 
-    terms = {1: [(S.arr_c, ENG_CHIP, T.cin, 1)],
-             2: [(S.arr_h, ENG_LINK, T.hin, 1)],
-             3: [(S.arr_c, ENG_CHIP, T.cin, 1), (S.arr_h, ENG_LINK, T.hin, 4)]}[rank]
+    terms = {1: [(S.arr_c, 2 * ENG_CHIP, [T.cx, T.cin], 1)],
+             2: [(S.arr_h, ENG_LINK, [T.hin], 1)],
+             3: [(S.arr_c, ENG_CHIP, [T.cin], 1), (S.arr_h, ENG_LINK, [T.hin], 4)]}[rank]
     py = [T.py0, T.py1, T.py2]
     ty = [S.t_y0, S.t_y1, S.t_y2]
-    for i, (sem, cnt, buf, p0) in enumerate(terms):
+    for i, (sem, cnt, bufs, p0) in enumerate(terms):
         te.wait_ge(sem, cnt)
-        last = i == len(terms) - 1
         for s in range(3):
-            mm = te.matmul(py[s][:, 0:B], P(p0 + s), buf[:], i == 0, last)
-            if last:
-                mm.then_inc(ty[s], 1)
+            for j, buf in enumerate(bufs):
+                first = i == 0 and j == 0
+                last = i == len(terms) - 1 and j == len(bufs) - 1
+                mm = te.matmul(py[s][:, 0:B], P(p0 + s), buf[:], first, last)
+                if last:
+                    mm.then_inc(ty[s], 1)
     ve.wait_ge(S.v_l1, 1)
     ve.wait_ge(S.v_l2, 1)
     for s in range(3):

@@ -15,6 +15,7 @@ SCRATCH = {
     "d0": ("sbuf", [128, B], _BF),
     "cin": ("sbuf", [128, B], _BF),
     "cx": ("sbuf", [128, B], _BF),
+    "hx": ("sbuf", [128, B], _BF),
     "hin": ("sbuf", [128, B], _BF),
     "rl0": ("sbuf", [128, B], _BF),
     "rl1": ("sbuf", [128, B], _BF),
@@ -28,8 +29,9 @@ SCRATCH = {
     "py1": ("psum", [128, 512], "float32"),
     "py2": ("psum", [128, 512], "float32"),
 }
-SEMAPHORES = ["ld_x", "ld_a", "ld_at", "t_l1", "t_l2", "v_l1", "v_l2", "v_m", "t_p1", "t_p2", "t_p3", "v_p1", "v_p2",
-              "v_p3", "t_d", "v_d", "t_y0", "t_y1", "t_y2", "v_y", "arr_c", "arr_h", "arr_r", "sent", "st"]
+SEMAPHORES = ["ld_x", "ld_xl", "ld_a", "ld_at", "t_l1", "t_l2", "v_l1", "v_l2", "v_m", "t_p1", "t_p2", "t_p3", "v_p1",
+              "v_p2", "v_p3", "t_d", "v_d", "t_y0", "t_y1", "t_y2", "v_y", "arr_c", "arr_h", "arr_x", "arr_r", "arr_e",
+              "sent", "st"]
 
 _SLOT = {1: 0, 2: 1, 3: 3, 4: 4, 5: 5, 6: 6}
 
@@ -65,11 +67,16 @@ def rank_program(g, core, T, topo):
 
     if core in relays:
         dst = cores[2 + relays.index(core)]
-        g.wait_ge(S.arr_r, 3 * ENG_CHIP)
+        rid, pid, _ = topo.addr(dst)
+        m = _engines(topo.mask(core, dst), ENG_LINK)
+        g.wait_ge(S.arr_e, ENG_CHIP)
+        g.remote_dma(out_ap=T.hx[:], in_ap=T.rlx[:], remote_sem=S.arr_x, local_sem=S.sent, pid=pid, routing_id=rid,
+                     dma_engine_mask=m)
+        g.wait_ge(S.arr_r, 2 * ENG_CHIP)
         g.remote_dma_fused([RemoteDMATransfer(
-            dst_ids=[_dst(topo, dst)], dma_engine_mask=_engines(topo.mask(core, dst), ENG_LINK), remote_sem=S.arr_h,
-            srcs=[T.rl0[:], T.rl1[:], T.rlx[:]], dsts=[T.hin[:]], alu_op=1)], local_sem=S.sent)
-        g.wait_ge(S.sent, ENG_LINK)
+            dst_ids=[_dst(topo, dst)], dma_engine_mask=m, remote_sem=S.arr_h,
+            srcs=[T.rl0[:], T.rl1[:]], dsts=[T.hin[:]], alu_op=1)], local_sem=S.sent)
+        g.wait_ge(S.sent, 2 * ENG_LINK)
         return
 
     rank = T.rank_of(core)
@@ -87,8 +94,9 @@ def rank_program(g, core, T, topo):
     wide = rank == 3
     w = 2 if wide else 1
 
-    sc.dma_start(T.xs[:], T.x[:]).then_inc(S.ld_x, 16)
+    sc.dma_start(xlast, T.x[:, 2 * B:3 * B]).then_inc(S.ld_xl, 16)
     sy.dma_start(A, T.a[:]).then_inc(S.ld_a, 16)
+    sc.dma_start(T.xs[:, 0:2 * B], T.x[:, 0:2 * B]).then_inc(S.ld_x, 16)
     sy.dma_start(T.ats[:], T.at[:]).then_inc(S.ld_at, 16)
 
     te.wait_ge(S.ld_a, 16)
@@ -116,6 +124,7 @@ def rank_program(g, core, T, topo):
 
     def v_carry():
         ve.wait_ge(S.t_l2, 1)
+        ve.wait_ge(S.ld_xl, 16)
         ve.tensor_tensor(l[2], T.pb[:, 0:B], xlast, AluOpType.add).then_inc(S.v_l2, 1)
 
     def v_m():
@@ -138,10 +147,10 @@ def rank_program(g, core, T, topo):
         ve.wait_ge(S.t_p3, 1)
         ve.tensor_copy(P(5, 2), T.pa[:, 0:2 * B]).then_inc(S.v_p3, 1)
 
-    def to_relays(src, land):
+    def to_relays(src, land, sem):
         m = topo.mask(core, relays[0]) & topo.mask(core, relays[1])
         g.remote_dma_fused([RemoteDMATransfer(
-            dst_ids=[_dst(topo, c) for c in relays], dma_engine_mask=_engines(m, ENG_CHIP), remote_sem=S.arr_r,
+            dst_ids=[_dst(topo, c) for c in relays], dma_engine_mask=_engines(m, ENG_CHIP), remote_sem=sem,
             srcs=[src], dsts=[land, land], alu_op=0)], local_sem=S.sent)
 
     def to_next(src, land):
@@ -156,10 +165,10 @@ def rank_program(g, core, T, topo):
         ve.wait_ge(S.t_d, 1)
         ve.tensor_copy(T.d0[:], T.py0[:, 0:B]).then_inc(S.v_d, 1)
         v_m()
-        g.wait_ge(S.ld_x, 16)
+        g.wait_ge(S.ld_xl, 16)
         to_next(xlast, T.cx[:])
         g.wait_ge(S.v_d, 1)
-        to_relays(T.d0[:], T.rl0[:])
+        to_relays(T.d0[:], T.rl0[:], S.arr_r)
         g.wait_ge(S.v_m, 1)
         to_next(T.mb[:], T.cin[:])
         g.wait_ge(S.sent, 3 * ENG_CHIP)
@@ -173,10 +182,10 @@ def rank_program(g, core, T, topo):
         return
 
     if rank == 1:
-        g.wait_ge(S.ld_x, 16)
-        to_relays(xlast, T.rlx[:])
+        g.wait_ge(S.ld_xl, 16)
+        to_relays(xlast, T.rlx[:], S.arr_e)
         g.wait_ge(S.v_m, 1)
-        to_relays(T.mb[:], T.rl1[:])
+        to_relays(T.mb[:], T.rl1[:], S.arr_r)
         g.wait_ge(S.sent, 2 * ENG_CHIP)
     elif rank == 2:
         g.wait_ge(S.v_l2, 1)
@@ -184,8 +193,8 @@ def rank_program(g, core, T, topo):
         g.wait_ge(S.sent, ENG_CHIP)
 
     terms = {1: [(S.arr_c, 2 * ENG_CHIP, [T.cx, T.cin], 1)],
-             2: [(S.arr_h, ENG_LINK, [T.hin], 1)],
-             3: [(S.arr_c, ENG_CHIP, [T.cin], 1), (S.arr_h, ENG_LINK, [T.hin], 4)]}[rank]
+             2: [(S.arr_x, ENG_LINK, [T.hx], 1), (S.arr_h, ENG_LINK, [T.hin], 1)],
+             3: [(S.arr_c, ENG_CHIP, [T.cin], 1), (S.arr_x, ENG_LINK, [T.hx], 4), (S.arr_h, ENG_LINK, [T.hin], 4)]}[rank]
     py = [T.py0, T.py1, T.py2]
     ty = [S.t_y0, S.t_y1, S.t_y2]
     for i, (sem, cnt, bufs, p0) in enumerate(terms):

@@ -1,8 +1,10 @@
 from concourse.bass import DstId, RemoteDMATransfer
-from concourse.mybir import AluOpType
+from concourse.mybir import AluOpType, ActivationFunctionType
 
 B = 128
+E = 8
 ENG_CHIP = 8
+ENG_R0 = 16
 ENG_LINK = 8
 
 _BF = "bfloat16"
@@ -12,32 +14,40 @@ SCRATCH = {
     "pw": ("sbuf", [128, 7 * B], _BF),
     "lb": ("sbuf", [128, 2 * B], _BF),
     "mb": ("sbuf", [128, B], _BF),
+    "wb": ("sbuf", [128, B], _BF),
     "d0": ("sbuf", [128, B], _BF),
     "cin": ("sbuf", [128, B], _BF),
     "cx": ("sbuf", [128, B], _BF),
-    "hx": ("sbuf", [128, B], _BF),
+    "hx": ("sbuf", [128, 2 * E], _BF),
+    "lq": ("sbuf", [128, 3 * B], _BF),
     "hin": ("sbuf", [128, B], _BF),
-    "rl0": ("sbuf", [128, B], _BF),
-    "rl1": ("sbuf", [128, B], _BF),
-    "rlx": ("sbuf", [128, B], _BF),
+    "hm": ("sbuf", [128, B], _BF),
+    "rl": ("sbuf", [128, B], _BF),
+    "xd": ("dram", [2, 128, E], _BF),
+    "rxd": ("dram", [128, E], _BF),
     "yb": ("sbuf", [128, 3 * B], _BF),
     "pa": ("psum", [128, 512], "float32"),
     "pb": ("psum", [128, 512], "float32"),
     "pc": ("psum", [128, 512], "float32"),
     "pd": ("psum", [128, 512], "float32"),
+    "pn": ("psum", [128, 512], "float32"),
     "py0": ("psum", [128, 512], "float32"),
     "py1": ("psum", [128, 512], "float32"),
     "py2": ("psum", [128, 512], "float32"),
 }
-SEMAPHORES = ["ld_x", "ld_xl", "ld_a", "ld_at", "t_l1", "t_l2", "v_l1", "v_l2", "v_m", "t_p1", "t_p2", "t_p3", "v_p1",
-              "v_p2", "v_p3", "t_d", "v_d", "t_y0", "t_y1", "t_y2", "v_y", "arr_c", "arr_h", "arr_x", "arr_r", "arr_e",
-              "sent", "st"]
+SEMAPHORES = ["ld_x", "ld_e", "ld_a", "ld_at", "t_l1", "t_l2", "v_l1", "v_l2", "v_m", "t_p1", "t_p2", "t_p3",
+              "v_p1", "v_p2", "v_p3", "t_w", "v_w", "t_d", "v_d", "t_n", "v_q", "t_y0", "t_y1", "t_y2", "v_y", "arr_c",
+              "arr_h", "arr_m", "arr_x", "arr_r", "arr_e", "sent", "st"]
 
 _SLOT = {1: 0, 2: 1, 3: 3, 4: 4, 5: 5, 6: 6}
 
 
+def _bits(mask):
+    return [b for b in range(mask.bit_length()) if (mask >> b) & 1]
+
+
 def _engines(mask, n):
-    bits = [b for b in range(mask.bit_length()) if (mask >> b) & 1]
+    bits = _bits(mask)
     m = 0
     for b in bits[::len(bits) // n][:n]:
         m |= 1 << b
@@ -47,11 +57,15 @@ def _engines(mask, n):
 def _relays(cores, topo):
     near = topo.chip(cores[1])
     idle = [c for c in range(topo.CHIPS * topo.CORES_PER_CHIP) if topo.chip(c) == near and c not in cores]
-    out = []
-    for dst in cores[2:]:
-        ok = [c for c in idle if topo.may_write(c, dst) and c not in out]
-        same = [c for c in ok if topo.die(c) == topo.die(dst)]
-        out.append((same or ok)[0])
+    used, out = [], []
+    for _ in range(2):
+        row = []
+        for dst in cores[2:]:
+            ok = [c for c in idle if topo.may_write(c, dst) and c not in used]
+            same = [c for c in ok if topo.die(c) == topo.die(dst)]
+            row.append((same or ok)[0])
+            used.append(row[-1])
+        out.append(row)
     return out
 
 
@@ -63,116 +77,93 @@ def _dst(topo, c):
 def rank_program(g, core, T, topo):
     cores = list(T.cores)
     S = T.sem
-    relays = _relays(cores, topo)
+    rel = _relays(cores, topo)
 
-    if core in relays:
-        dst = cores[2 + relays.index(core)]
-        rid, pid, _ = topo.addr(dst)
-        m = _engines(topo.mask(core, dst), ENG_LINK)
-        g.wait_ge(S.arr_e, ENG_CHIP)
-        g.remote_dma(out_ap=T.hx[:], in_ap=T.rlx[:], remote_sem=S.arr_x, local_sem=S.sent, pid=pid, routing_id=rid,
-                     dma_engine_mask=m)
-        g.wait_ge(S.arr_r, 2 * ENG_CHIP)
-        g.remote_dma_fused([RemoteDMATransfer(
-            dst_ids=[_dst(topo, dst)], dma_engine_mask=m, remote_sem=S.arr_h,
-            srcs=[T.rl0[:], T.rl1[:]], dsts=[T.hin[:]], alu_op=1)], local_sem=S.sent)
-        g.wait_ge(S.sent, 2 * ENG_LINK)
-        return
+    for k in range(2):
+        if core in rel[k]:
+            dst = cores[2 + rel[k].index(core)]
+            rid, pid, _ = topo.addr(dst)
+            m = _engines(topo.mask(core, dst), ENG_LINK)
+            g.wait_ge(S.arr_e, ENG_CHIP // 2)
+            g.remote_dma(out_ap=T.hx[:, k * E:(k + 1) * E], in_ap=T.rxd[:], remote_sem=S.arr_x, local_sem=S.sent,
+                         pid=pid, routing_id=rid, dma_engine_mask=m)
+            g.wait_ge(S.arr_r, ENG_R0 if k == 0 else ENG_CHIP)
+            g.remote_dma(out_ap=(T.hin[:] if k == 0 else T.hm[:]), in_ap=T.rl[:],
+                         remote_sem=(S.arr_h if k == 0 else S.arr_m), local_sem=S.sent,
+                         pid=pid, routing_id=rid, dma_engine_mask=m)
+            g.wait_ge(S.sent, 2 * ENG_LINK)
+            return
 
     rank = T.rank_of(core)
     if rank is None:
         return
     te, ve, sy, sc = g.tensor, g.vector, g.sync, g.scalar
+    COPY = ActivationFunctionType.Copy
 
     def P(k, n=1):
         return T.pw[:, _SLOT[k] * B:(_SLOT[k] + n) * B]
 
+    def L(s, c0=0, c1=B):
+        return T.xs[:, c0:c1] if s == 0 else T.lb[:, (s - 1) * B + c0:(s - 1) * B + c1]
+
     A = P(1)
     AT2 = T.pw[:, 2 * B:3 * B]
-    l = [T.xs[:, 0:B], T.lb[:, 0:B], T.lb[:, B:2 * B]]
+    l = [L(0), L(1), L(2)]
     xlast = T.xs[:, 2 * B:3 * B]
     wide = rank == 3
-    w = 2 if wide else 1
 
-    sc.dma_start(xlast, T.x[:, 2 * B:3 * B]).then_inc(S.ld_xl, 16)
-    sy.dma_start(A, T.a[:]).then_inc(S.ld_a, 16)
-    sc.dma_start(T.xs[:, 0:2 * B], T.x[:, 0:2 * B]).then_inc(S.ld_x, 16)
-    sy.dma_start(T.ats[:], T.at[:]).then_inc(S.ld_at, 16)
-
-    te.wait_ge(S.ld_a, 16)
-    te.wait_ge(S.ld_x, 16)
-    te.matmul(T.pa[:, 0:B], A, l[0], True, True).then_inc(S.t_l1, 1)
-    te.wait_ge(S.ld_at, 16)
-    te.matmul(T.pc[:, 0:B], T.ats[:], A, True, True).then_inc(S.t_p1, 1)
-    if wide:
-        te.matmul(T.pc[:, B:2 * B], A, T.ats[:], True, True).then_inc(S.t_p1, 1)
-    te.wait_ge(S.v_l1, 1)
-    te.matmul(T.pb[:, 0:B], A, l[1], True, True).then_inc(S.t_l2, 1)
-    te.wait_ge(S.v_p1, 1)
-    if wide:
-        te.matmul(T.pd[:, 0:2 * B], AT2, P(1, 2), True, True).then_inc(S.t_p2, 1)
-        te.wait_ge(S.v_p2, 1)
-        te.matmul(T.pa[:, 0:2 * B], AT2, P(3, 2), True, True).then_inc(S.t_p3, 1)
-        te.wait_ge(S.v_p3, 1)
-    else:
-        te.matmul(T.pd[:, 0:B], T.ats[:], P(2), True, True).then_inc(S.t_p2, 1)
-        te.wait_ge(S.v_p2, 1)
-
-    def v_square():
-        ve.wait_ge(S.t_p1, w)
-        ve.tensor_copy(T.pw[:, B:(1 + w) * B], T.pc[:, 0:w * B]).then_inc(S.v_p1, 1)
-
-    def v_carry():
-        ve.wait_ge(S.t_l2, 1)
-        ve.wait_ge(S.ld_xl, 16)
-        ve.tensor_tensor(l[2], T.pb[:, 0:B], xlast, AluOpType.add).then_inc(S.v_l2, 1)
-
-    def v_m():
-        ve.wait_ge(S.t_l2, 1)
-        ve.tensor_copy(T.mb[:], T.pb[:, 0:B]).then_inc(S.v_m, 1)
-
-    ve.wait_ge(S.ld_x, 16)
-    ve.wait_ge(S.t_l1, 1)
-    ve.tensor_tensor(l[1], T.pa[:, 0:B], T.xs[:, B:2 * B], AluOpType.add).then_inc(S.v_l1, 1)
-    if rank == 1:
-        v_m()
-        v_carry()
-        v_square()
-    else:
-        v_square()
-        v_carry()
-    ve.wait_ge(S.t_p2, 1)
-    ve.tensor_copy(P(3, w), T.pd[:, 0:w * B]).then_inc(S.v_p2, 1)
-    if wide:
-        ve.wait_ge(S.t_p3, 1)
-        ve.tensor_copy(P(5, 2), T.pa[:, 0:2 * B]).then_inc(S.v_p3, 1)
-
-    def to_relays(src, land, sem):
-        m = topo.mask(core, relays[0]) & topo.mask(core, relays[1])
+    def to_relays(k, src, neng):
+        m = topo.mask(core, rel[k][0]) & topo.mask(core, rel[k][1])
         g.remote_dma_fused([RemoteDMATransfer(
-            dst_ids=[_dst(topo, c) for c in relays], dma_engine_mask=_engines(m, ENG_CHIP), remote_sem=sem,
-            srcs=[src], dsts=[land, land], alu_op=0)], local_sem=S.sent)
+            dst_ids=[_dst(topo, c) for c in rel[k]], dma_engine_mask=_engines(m, neng), remote_sem=S.arr_r,
+            srcs=[src], dsts=[T.rl[:], T.rl[:]], alu_op=0)], local_sem=S.sent)
 
-    def to_next(src, land):
+    def to_next(src, land, neng):
         dst = cores[rank + 1]
         rid, pid, _ = topo.addr(dst)
         g.remote_dma(out_ap=land, in_ap=src, remote_sem=S.arr_c, local_sem=S.sent, pid=pid, routing_id=rid,
-                     dma_engine_mask=_engines(topo.mask(core, dst), ENG_CHIP))
+                     dma_engine_mask=_engines(topo.mask(core, dst), neng))
+
+    if rank == 1:
+        sc.dma_start(T.xd[0], T.x[:, 2 * B:2 * B + E]).then_inc(S.ld_e, 16)
+        sy.dma_start(T.xd[1], T.x[:, 2 * B + E:2 * B + 2 * E]).then_inc(S.ld_e, 16)
+    sc.dma_start(T.xs[:], T.x[:]).then_inc(S.ld_x, 16)
+    sy.dma_start(A, T.a[:]).then_inc(S.ld_a, 16)
+    (sy if rank == 1 else sc).dma_start(T.ats[:], T.at[:]).then_inc(S.ld_at, 16)
 
     if rank == 0:
-        te.wait_ge(S.v_l2, 1)
-        te.matmul(T.py0[:, 0:B], P(3), l[2], True, True).then_inc(S.t_d, 1)
+        te.wait_ge(S.ld_a, 16)
+        te.wait_ge(S.ld_x, 16)
+        te.matmul(T.pa[:, 0:B], A, l[0], True, True).then_inc(S.t_l1, 1)
+        te.wait_ge(S.ld_at, 16)
+        te.matmul(T.pc[:, 0:B], T.ats[:], A, True, True).then_inc(S.t_p1, 1)
+        te.matmul(T.pd[:, 0:B], A, xlast, True, False)
+        te.wait_ge(S.v_l1, 1)
+        te.wait_ge(S.v_p1, 1)
+        te.matmul(T.pd[:, 0:B], P(2), l[1], False, True).then_inc(S.t_w, 1)
+        te.matmul(T.pb[:, 0:B], A, l[1], True, True).then_inc(S.t_l2, 1)
+        te.wait_ge(S.v_w, 1)
+        te.matmul(T.py0[:, 0:B], P(2), T.wb[:], True, True).then_inc(S.t_d, 1)
+        sc.wait_ge(S.t_p1, 1)
+        sc.activation(P(2), T.pc[:, 0:B], COPY).then_inc(S.v_p1, 1)
+        ve.wait_ge(S.ld_x, 16)
+        ve.wait_ge(S.t_l1, 1)
+        ve.tensor_tensor(l[1], T.pa[:, 0:B], T.xs[:, B:2 * B], AluOpType.add).then_inc(S.v_l1, 1)
+        ve.wait_ge(S.t_w, 1)
+        ve.tensor_copy(T.wb[:], T.pd[:, 0:B]).then_inc(S.v_w, 1)
         ve.wait_ge(S.t_d, 1)
         ve.tensor_copy(T.d0[:], T.py0[:, 0:B]).then_inc(S.v_d, 1)
-        v_m()
-        g.wait_ge(S.ld_xl, 16)
-        to_next(xlast, T.cx[:])
+        ve.wait_ge(S.t_l2, 1)
+        ve.tensor_copy(T.mb[:], T.pb[:, 0:B]).then_inc(S.v_m, 1)
+        ve.tensor_tensor(l[2], T.pb[:, 0:B], xlast, AluOpType.add).then_inc(S.v_l2, 1)
+        g.wait_ge(S.ld_x, 16)
+        to_next(xlast, T.cx[:], ENG_R0)
         g.wait_ge(S.v_d, 1)
-        to_relays(T.d0[:], T.rl0[:], S.arr_r)
+        to_relays(0, T.d0[:], ENG_R0)
         g.wait_ge(S.v_m, 1)
-        to_next(T.mb[:], T.cin[:])
-        g.wait_ge(S.sent, 3 * ENG_CHIP)
-        sy.wait_ge(S.sent, 3 * ENG_CHIP)
+        to_next(T.mb[:], T.cin[:], ENG_R0)
+        g.wait_ge(S.sent, 3 * ENG_R0)
+        sy.wait_ge(S.sent, 3 * ENG_R0)
         sy.wait_ge(S.ld_x, 16)
         sy.wait_ge(S.v_l1, 1)
         sy.wait_ge(S.v_l2, 1)
@@ -181,36 +172,104 @@ def rank_program(g, core, T, topo):
         sy.wait_ge(S.st, 32)
         return
 
+    te.wait_ge(S.ld_a, 16)
+    te.wait_ge(S.ld_x, 16)
+    te.matmul(T.pa[:, 0:B], A, l[0], True, True).then_inc(S.t_l1, 1)
+    if wide:
+        te.wait_ge(S.ld_at, 16)
+        te.matmul(T.pc[:, 0:B], T.ats[:], A, True, True).then_inc(S.t_p1, 1)
+        te.matmul(T.pc[:, B:2 * B], A, T.ats[:], True, True).then_inc(S.t_p1, 1)
+        te.wait_ge(S.v_l1, 1)
+        te.matmul(T.pb[:, 0:B], A, l[1], True, True).then_inc(S.t_l2, 1)
+        te.wait_ge(S.v_p1, 1)
+        te.matmul(T.pd[:, 0:2 * B], AT2, P(1, 2), True, True).then_inc(S.t_p2, 1)
+        te.wait_ge(S.v_p2, 1)
+        te.matmul(T.pa[:, 0:2 * B], AT2, P(3, 2), True, True).then_inc(S.t_p3, 1)
+        te.wait_ge(S.v_p3, 1)
+    else:
+        te.wait_ge(S.v_l1, 1)
+        te.matmul(T.pb[:, 0:B], A, l[1], True, True).then_inc(S.t_l2, 1)
+        te.wait_ge(S.ld_at, 16)
+        te.matmul(T.pc[:, 0:B], T.ats[:], A, True, True).then_inc(S.t_p1, 1)
+        te.wait_ge(S.v_p1, 1)
+        te.matmul(T.pd[:, 0:B], T.ats[:], P(2), True, True).then_inc(S.t_p2, 1)
+        te.wait_ge(S.v_p2, 1)
+        sc.wait_ge(S.t_p1, 1)
+        sc.activation(P(2), T.pc[:, 0:B], COPY).then_inc(S.v_p1, 1)
+        sc.wait_ge(S.t_p2, 1)
+        sc.activation(P(3), T.pd[:, 0:B], COPY).then_inc(S.v_p2, 1)
+
+    ve.wait_ge(S.ld_x, 16)
+    ve.wait_ge(S.t_l1, 1)
+    ve.tensor_tensor(l[1], T.pa[:, 0:B], T.xs[:, B:2 * B], AluOpType.add).then_inc(S.v_l1, 1)
+    if wide:
+        ve.wait_ge(S.t_p1, 2)
+        ve.tensor_copy(T.pw[:, B:3 * B], T.pc[:, 0:2 * B]).then_inc(S.v_p1, 1)
+    ve.wait_ge(S.t_l2, 1)
     if rank == 1:
-        g.wait_ge(S.ld_xl, 16)
-        to_relays(xlast, T.rlx[:], S.arr_e)
-        g.wait_ge(S.v_m, 1)
-        to_relays(T.mb[:], T.rl1[:], S.arr_r)
+        ve.tensor_tensor(T.mb[:, 2 * E:B], T.pb[:, 2 * E:B], T.xs[:, 2 * B + 2 * E:3 * B],
+                         AluOpType.add).then_inc(S.v_m, 1)
+        ve.tensor_copy(T.mb[:, 0:2 * E], T.pb[:, 0:2 * E]).then_inc(S.v_m, 1)
+    ve.tensor_tensor(l[2], T.pb[:, 0:B], xlast, AluOpType.add).then_inc(S.v_l2, 1)
+    if wide:
+        ve.wait_ge(S.t_p2, 1)
+        ve.tensor_copy(P(3, 2), T.pd[:, 0:2 * B]).then_inc(S.v_p2, 1)
+        ve.wait_ge(S.t_p3, 1)
+        ve.tensor_copy(P(5, 2), T.pa[:, 0:2 * B]).then_inc(S.v_p3, 1)
+
+    if rank == 1:
+        m = topo.mask(core, rel[0][0])
+        for c in rel[0] + rel[1]:
+            m &= topo.mask(core, c)
+        bits = _bits(_engines(m, ENG_CHIP))
+        half = [sum(1 << b for b in bits[0::2]), sum(1 << b for b in bits[1::2])]
+        g.wait_ge(S.ld_e, 32)
+        g.remote_dma_fused([RemoteDMATransfer(
+            dst_ids=[_dst(topo, c) for c in rel[k]], dma_engine_mask=half[k], remote_sem=S.arr_e,
+            srcs=[T.xd[k]], dsts=[T.rxd[:], T.rxd[:]], alu_op=0) for k in range(2)], local_sem=S.sent)
+        g.wait_ge(S.v_m, 2)
+        to_relays(1, T.mb[:], ENG_CHIP)
         g.wait_ge(S.sent, 2 * ENG_CHIP)
     elif rank == 2:
         g.wait_ge(S.v_l2, 1)
-        to_next(l[2], T.cin[:])
+        to_next(l[2], T.cin[:], ENG_CHIP)
         g.wait_ge(S.sent, ENG_CHIP)
 
-    terms = {1: [(S.arr_c, 2 * ENG_CHIP, [T.cx, T.cin], 1)],
-             2: [(S.arr_x, ENG_LINK, [T.hx], 1), (S.arr_h, ENG_LINK, [T.hin], 1)],
-             3: [(S.arr_c, ENG_CHIP, [T.cin], 1), (S.arr_x, ENG_LINK, [T.hx], 4), (S.arr_h, ENG_LINK, [T.hin], 4)]}[rank]
+    far = lambda p: [(S.arr_x, 2 * ENG_LINK, None, p), (S.arr_m, ENG_LINK, [T.hm], p), (S.arr_h, ENG_LINK, [T.hin], p)]
+    terms = {1: [(S.arr_c, 2 * ENG_R0, [T.cx, T.cin], 1)],
+             2: far(1),
+             3: [(S.arr_c, ENG_CHIP, [T.cin], 1)] + far(4)}[rank]
     py = [T.py0, T.py1, T.py2]
     ty = [S.t_y0, S.t_y1, S.t_y2]
+    first = True
     for i, (sem, cnt, bufs, p0) in enumerate(terms):
         te.wait_ge(sem, cnt)
-        for s in range(3):
-            for j, buf in enumerate(bufs):
-                first = i == 0 and j == 0
-                last = i == len(terms) - 1 and j == len(bufs) - 1
+        if bufs is None:
+            for s in range(3):
+                te.matmul(T.pn[:, s * 2 * E:(s + 1) * 2 * E], P(p0 + s), T.hx[:], True, True).then_inc(S.t_n, 1)
+            continue
+        for j, buf in enumerate(bufs):
+            last = i == len(terms) - 1 and j == len(bufs) - 1
+            for s in range(3):
                 mm = te.matmul(py[s][:, 0:B], P(p0 + s), buf[:], first, last)
                 if last:
                     mm.then_inc(ty[s], 1)
+            first = False
     ve.wait_ge(S.v_l1, 1)
     ve.wait_ge(S.v_l2, 1)
+    base = l
+    if rank >= 2:
+        base = [T.lq[:, s * B:(s + 1) * B] for s in range(3)]
+        for s in range(3):
+            ve.tensor_copy(T.lq[:, s * B + 2 * E:(s + 1) * B], L(s, 2 * E, B)).then_inc(S.v_q, 1)
+        ve.wait_ge(S.t_n, 3)
+        for s in range(3):
+            ve.tensor_tensor(T.lq[:, s * B:s * B + 2 * E], T.pn[:, s * 2 * E:(s + 1) * 2 * E], L(s, 0, 2 * E),
+                             AluOpType.add).then_inc(S.v_q, 1)
+        ve.wait_ge(S.v_q, 6)
     for s in range(3):
         ve.wait_ge(ty[s], 1)
-        ve.tensor_tensor(T.yb[:, s * B:(s + 1) * B], py[s][:, 0:B], l[s], AluOpType.add).then_inc(S.v_y, 1)
+        ve.tensor_tensor(T.yb[:, s * B:(s + 1) * B], py[s][:, 0:B], base[s], AluOpType.add).then_inc(S.v_y, 1)
     sy.wait_ge(S.v_y, 3)
     sy.dma_start(T.y[:], T.yb[:]).then_inc(S.st, 16)
     sy.wait_ge(S.st, 16)

from concourse.bass import DstId, RemoteDMATransfer
from concourse.mybir import AluOpType, ActivationFunctionType

B = 128
E = 8
ENG_CHIP = 8
ENG_R0 = 16
ENG_LINK = 8

_BF = "bfloat16"
SCRATCH = {
    "xs": ("sbuf", [128, 3 * B], _BF),
    "ats": ("sbuf", [128, B], _BF),
    "pw": ("sbuf", [128, 7 * B], _BF),
    "lb": ("sbuf", [128, 2 * B], _BF),
    "mb": ("sbuf", [128, B], _BF),
    "wb": ("sbuf", [128, B], _BF),
    "d0": ("sbuf", [128, B], _BF),
    "cin": ("sbuf", [128, B], _BF),
    "cx": ("sbuf", [128, B], _BF),
    "hx": ("sbuf", [128, 2 * E], _BF),
    "lq": ("sbuf", [128, 3 * B], _BF),
    "hin": ("sbuf", [128, B], _BF),
    "hm": ("sbuf", [128, B], _BF),
    "rl": ("sbuf", [128, B], _BF),
    "xd": ("dram", [2, 128, E], _BF),
    "rxd": ("dram", [128, E], _BF),
    "yb": ("sbuf", [128, 3 * B], _BF),
    "pa": ("psum", [128, 512], "float32"),
    "pb": ("psum", [128, 512], "float32"),
    "pc": ("psum", [128, 512], "float32"),
    "pd": ("psum", [128, 512], "float32"),
    "pn": ("psum", [128, 512], "float32"),
    "py0": ("psum", [128, 512], "float32"),
    "py1": ("psum", [128, 512], "float32"),
    "py2": ("psum", [128, 512], "float32"),
}
SEMAPHORES = ["ld_x", "ld_e", "ld_a", "ld_at", "t_l1", "t_l2", "v_l1", "v_l2", "v_m", "t_p1", "t_p2", "t_p3",
              "v_p1", "v_p2", "v_p3", "t_w", "v_w", "t_d", "v_d", "t_n", "v_q", "t_y0", "t_y1", "t_y2", "v_y", "arr_c",
              "arr_h", "arr_m", "arr_x", "arr_r", "arr_e", "sent", "st"]

_SLOT = {1: 0, 2: 1, 3: 3, 4: 4, 5: 5, 6: 6}


def _bits(mask):
    return [b for b in range(mask.bit_length()) if (mask >> b) & 1]


def _engines(mask, n):
    bits = _bits(mask)
    m = 0
    for b in bits[::len(bits) // n][:n]:
        m |= 1 << b
    return m


def _relays(cores, topo):
    near = topo.chip(cores[1])
    idle = [c for c in range(topo.CHIPS * topo.CORES_PER_CHIP) if topo.chip(c) == near and c not in cores]
    used, out = [], []
    for _ in range(2):
        row = []
        for dst in cores[2:]:
            ok = [c for c in idle if topo.may_write(c, dst) and c not in used]
            same = [c for c in ok if topo.die(c) == topo.die(dst)]
            row.append((same or ok)[0])
            used.append(row[-1])
        out.append(row)
    return out


def _dst(topo, c):
    rid, pid, _ = topo.addr(c)
    return DstId(rid=rid, pnc=pid)


def rank_program(g, core, T, topo):
    cores = list(T.cores)
    S = T.sem
    rel = _relays(cores, topo)

    for k in range(2):
        if core in rel[k]:
            dst = cores[2 + rel[k].index(core)]
            rid, pid, _ = topo.addr(dst)
            m = _engines(topo.mask(core, dst), ENG_LINK)
            g.wait_ge(S.arr_e, ENG_CHIP // 2)
            g.remote_dma(out_ap=T.hx[:, k * E:(k + 1) * E], in_ap=T.rxd[:], remote_sem=S.arr_x, local_sem=S.sent,
                         pid=pid, routing_id=rid, dma_engine_mask=m)
            g.wait_ge(S.arr_r, ENG_R0 if k == 0 else ENG_CHIP)
            g.remote_dma(out_ap=(T.hin[:] if k == 0 else T.hm[:]), in_ap=T.rl[:],
                         remote_sem=(S.arr_h if k == 0 else S.arr_m), local_sem=S.sent,
                         pid=pid, routing_id=rid, dma_engine_mask=m)
            g.wait_ge(S.sent, 2 * ENG_LINK)
            return

    rank = T.rank_of(core)
    if rank is None:
        return
    te, ve, sy, sc = g.tensor, g.vector, g.sync, g.scalar
    COPY = ActivationFunctionType.Copy

    def P(k, n=1):
        return T.pw[:, _SLOT[k] * B:(_SLOT[k] + n) * B]

    def L(s, c0=0, c1=B):
        return T.xs[:, c0:c1] if s == 0 else T.lb[:, (s - 1) * B + c0:(s - 1) * B + c1]

    A = P(1)
    AT2 = T.pw[:, 2 * B:3 * B]
    l = [L(0), L(1), L(2)]
    xlast = T.xs[:, 2 * B:3 * B]
    wide = rank == 3

    def to_relays(k, src, neng):
        m = topo.mask(core, rel[k][0]) & topo.mask(core, rel[k][1])
        g.remote_dma_fused([RemoteDMATransfer(
            dst_ids=[_dst(topo, c) for c in rel[k]], dma_engine_mask=_engines(m, neng), remote_sem=S.arr_r,
            srcs=[src], dsts=[T.rl[:], T.rl[:]], alu_op=0)], local_sem=S.sent)

    def to_next(src, land, neng):
        dst = cores[rank + 1]
        rid, pid, _ = topo.addr(dst)
        g.remote_dma(out_ap=land, in_ap=src, remote_sem=S.arr_c, local_sem=S.sent, pid=pid, routing_id=rid,
                     dma_engine_mask=_engines(topo.mask(core, dst), neng))

    if rank == 1:
        sc.dma_start(T.xd[0], T.x[:, 2 * B:2 * B + E]).then_inc(S.ld_e, 16)
        sy.dma_start(T.xd[1], T.x[:, 2 * B + E:2 * B + 2 * E]).then_inc(S.ld_e, 16)
    sc.dma_start(T.xs[:], T.x[:]).then_inc(S.ld_x, 16)
    sy.dma_start(A, T.a[:]).then_inc(S.ld_a, 16)
    (sy if rank == 1 else sc).dma_start(T.ats[:], T.at[:]).then_inc(S.ld_at, 16)

    if rank == 0:
        te.wait_ge(S.ld_a, 16)
        te.wait_ge(S.ld_x, 16)
        te.matmul(T.pa[:, 0:B], A, l[0], True, True).then_inc(S.t_l1, 1)
        te.wait_ge(S.ld_at, 16)
        te.matmul(T.pc[:, 0:B], T.ats[:], A, True, True).then_inc(S.t_p1, 1)
        te.matmul(T.pd[:, 0:B], A, xlast, True, False)
        te.wait_ge(S.v_l1, 1)
        te.wait_ge(S.v_p1, 1)
        te.matmul(T.pd[:, 0:B], P(2), l[1], False, True).then_inc(S.t_w, 1)
        te.matmul(T.pb[:, 0:B], A, l[1], True, True).then_inc(S.t_l2, 1)
        te.wait_ge(S.v_w, 1)
        te.matmul(T.py0[:, 0:B], P(2), T.wb[:], True, True).then_inc(S.t_d, 1)
        sc.wait_ge(S.t_p1, 1)
        sc.activation(P(2), T.pc[:, 0:B], COPY).then_inc(S.v_p1, 1)
        ve.wait_ge(S.ld_x, 16)
        ve.wait_ge(S.t_l1, 1)
        ve.tensor_tensor(l[1], T.pa[:, 0:B], T.xs[:, B:2 * B], AluOpType.add).then_inc(S.v_l1, 1)
        ve.wait_ge(S.t_w, 1)
        ve.tensor_copy(T.wb[:], T.pd[:, 0:B]).then_inc(S.v_w, 1)
        ve.wait_ge(S.t_d, 1)
        ve.tensor_copy(T.d0[:], T.py0[:, 0:B]).then_inc(S.v_d, 1)
        ve.wait_ge(S.t_l2, 1)
        ve.tensor_copy(T.mb[:], T.pb[:, 0:B]).then_inc(S.v_m, 1)
        ve.tensor_tensor(l[2], T.pb[:, 0:B], xlast, AluOpType.add).then_inc(S.v_l2, 1)
        g.wait_ge(S.ld_x, 16)
        to_next(xlast, T.cx[:], ENG_R0)
        g.wait_ge(S.v_d, 1)
        to_relays(0, T.d0[:], ENG_R0)
        g.wait_ge(S.v_m, 1)
        to_next(T.mb[:], T.cin[:], ENG_R0)
        g.wait_ge(S.sent, 3 * ENG_R0)
        sy.wait_ge(S.sent, 3 * ENG_R0)
        sy.wait_ge(S.ld_x, 16)
        sy.wait_ge(S.v_l1, 1)
        sy.wait_ge(S.v_l2, 1)
        sy.dma_start(T.y[:, 0:B], l[0]).then_inc(S.st, 16)
        sy.dma_start(T.y[:, B:3 * B], T.lb[:]).then_inc(S.st, 16)
        sy.wait_ge(S.st, 32)
        return

    te.wait_ge(S.ld_a, 16)
    te.wait_ge(S.ld_x, 16)
    te.matmul(T.pa[:, 0:B], A, l[0], True, True).then_inc(S.t_l1, 1)
    if wide:
        te.wait_ge(S.ld_at, 16)
        te.matmul(T.pc[:, 0:B], T.ats[:], A, True, True).then_inc(S.t_p1, 1)
        te.matmul(T.pc[:, B:2 * B], A, T.ats[:], True, True).then_inc(S.t_p1, 1)
        te.wait_ge(S.v_l1, 1)
        te.matmul(T.pb[:, 0:B], A, l[1], True, True).then_inc(S.t_l2, 1)
        te.wait_ge(S.v_p1, 1)
        te.matmul(T.pd[:, 0:2 * B], AT2, P(1, 2), True, True).then_inc(S.t_p2, 1)
        te.wait_ge(S.v_p2, 1)
        te.matmul(T.pa[:, 0:2 * B], AT2, P(3, 2), True, True).then_inc(S.t_p3, 1)
        te.wait_ge(S.v_p3, 1)
    else:
        te.wait_ge(S.v_l1, 1)
        te.matmul(T.pb[:, 0:B], A, l[1], True, True).then_inc(S.t_l2, 1)
        te.wait_ge(S.ld_at, 16)
        te.matmul(T.pc[:, 0:B], T.ats[:], A, True, True).then_inc(S.t_p1, 1)
        te.wait_ge(S.v_p1, 1)
        te.matmul(T.pd[:, 0:B], T.ats[:], P(2), True, True).then_inc(S.t_p2, 1)
        te.wait_ge(S.v_p2, 1)
        sc.wait_ge(S.t_p1, 1)
        sc.activation(P(2), T.pc[:, 0:B], COPY).then_inc(S.v_p1, 1)
        sc.wait_ge(S.t_p2, 1)
        sc.activation(P(3), T.pd[:, 0:B], COPY).then_inc(S.v_p2, 1)

    ve.wait_ge(S.ld_x, 16)
    ve.wait_ge(S.t_l1, 1)
    ve.tensor_tensor(l[1], T.pa[:, 0:B], T.xs[:, B:2 * B], AluOpType.add).then_inc(S.v_l1, 1)
    if wide:
        ve.wait_ge(S.t_p1, 2)
        ve.tensor_copy(T.pw[:, B:3 * B], T.pc[:, 0:2 * B]).then_inc(S.v_p1, 1)
    ve.wait_ge(S.t_l2, 1)
    if rank == 1:
        ve.tensor_tensor(T.mb[:, 2 * E:B], T.pb[:, 2 * E:B], T.xs[:, 2 * B + 2 * E:3 * B],
                         AluOpType.add).then_inc(S.v_m, 1)
        ve.tensor_copy(T.mb[:, 0:2 * E], T.pb[:, 0:2 * E]).then_inc(S.v_m, 1)
    ve.tensor_tensor(l[2], T.pb[:, 0:B], xlast, AluOpType.add).then_inc(S.v_l2, 1)
    if wide:
        ve.wait_ge(S.t_p2, 1)
        ve.tensor_copy(P(3, 2), T.pd[:, 0:2 * B]).then_inc(S.v_p2, 1)
        ve.wait_ge(S.t_p3, 1)
        ve.tensor_copy(P(5, 2), T.pa[:, 0:2 * B]).then_inc(S.v_p3, 1)

    if rank == 1:
        m = topo.mask(core, rel[0][0])
        for c in rel[0] + rel[1]:
            m &= topo.mask(core, c)
        bits = _bits(_engines(m, ENG_CHIP))
        half = [sum(1 << b for b in bits[0::2]), sum(1 << b for b in bits[1::2])]
        g.wait_ge(S.ld_e, 32)
        g.remote_dma_fused([RemoteDMATransfer(
            dst_ids=[_dst(topo, c) for c in rel[k]], dma_engine_mask=half[k], remote_sem=S.arr_e,
            srcs=[T.xd[k]], dsts=[T.rxd[:], T.rxd[:]], alu_op=0) for k in range(2)], local_sem=S.sent)
        g.wait_ge(S.v_m, 2)
        to_relays(1, T.mb[:], ENG_CHIP)
        g.wait_ge(S.sent, 2 * ENG_CHIP)
    elif rank == 2:
        g.wait_ge(S.v_l2, 1)
        to_next(l[2], T.cin[:], ENG_CHIP)
        g.wait_ge(S.sent, ENG_CHIP)

    far = lambda p: [(S.arr_x, 2 * ENG_LINK, None, p), (S.arr_m, ENG_LINK, [T.hm], p), (S.arr_h, ENG_LINK, [T.hin], p)]
    terms = {1: [(S.arr_c, 2 * ENG_R0, [T.cx, T.cin], 1)],
             2: far(1),
             3: [(S.arr_c, ENG_CHIP, [T.cin], 1)] + far(4)}[rank]
    py = [T.py0, T.py1, T.py2]
    ty = [S.t_y0, S.t_y1, S.t_y2]
    first = True
    for i, (sem, cnt, bufs, p0) in enumerate(terms):
        te.wait_ge(sem, cnt)
        if bufs is None:
            for s in range(3):
                te.matmul(T.pn[:, s * 2 * E:(s + 1) * 2 * E], P(p0 + s), T.hx[:], True, True).then_inc(S.t_n, 1)
            continue
        for j, buf in enumerate(bufs):
            last = i == len(terms) - 1 and j == len(bufs) - 1
            for s in range(3):
                mm = te.matmul(py[s][:, 0:B], P(p0 + s), buf[:], first, last)
                if last:
                    mm.then_inc(ty[s], 1)
            first = False
    ve.wait_ge(S.v_l1, 1)
    ve.wait_ge(S.v_l2, 1)
    base = l
    if rank >= 2:
        base = [T.lq[:, s * B:(s + 1) * B] for s in range(3)]
        for s in range(3):
            ve.tensor_copy(T.lq[:, s * B + 2 * E:(s + 1) * B], L(s, 2 * E, B)).then_inc(S.v_q, 1)
        ve.wait_ge(S.t_n, 3)
        for s in range(3):
            ve.tensor_tensor(T.lq[:, s * B:s * B + 2 * E], T.pn[:, s * 2 * E:(s + 1) * 2 * E], L(s, 0, 2 * E),
                             AluOpType.add).then_inc(S.v_q, 1)
        ve.wait_ge(S.v_q, 6)
    for s in range(3):
        ve.wait_ge(ty[s], 1)
        ve.tensor_tensor(T.yb[:, s * B:(s + 1) * B], py[s][:, 0:B], base[s], AluOpType.add).then_inc(S.v_y, 1)
    sy.wait_ge(S.v_y, 3)
    sy.dma_start(T.y[:], T.yb[:]).then_inc(S.st, 16)
    sy.wait_ge(S.st, 16)
